import numpy as np, ml_dtypes
CORES = [32,160,288,416,80,208,336,464]
N = 8
TK = 32
def silu(z): return z / (1.0 + np.exp(-z))
def setup_inputs(rng):
    return {"x": rng.standard_normal((N, 128, TK), dtype=np.float32).astype(ml_dtypes.bfloat16), "w1": (rng.standard_normal((N, 128, 128), dtype=np.float32) / 8).astype(ml_dtypes.bfloat16), "w3": (rng.standard_normal((N, 128, 128), dtype=np.float32) / 8).astype(ml_dtypes.bfloat16), "w2": (rng.standard_normal((N, 128, 128), dtype=np.float32) / 8).astype(ml_dtypes.bfloat16)}
def setup_inputs_big(rng):
    d = setup_inputs(rng)
    for k in ("x",): d[k] = (d[k].astype(np.float32) * 1024.0).astype(d[k].dtype)
    return d
def setup_inputs_small(rng):
    d = setup_inputs(rng)
    for k in ("x",): d[k] = (d[k].astype(np.float32) * (1 / 1024.0)).astype(d[k].dtype)
    return d
def setup_inputs_apart(rng):
    d = setup_inputs(rng)
    f = (10.0 ** rng.permutation(np.linspace(-1.5, 1.5, N))).astype(np.float32).reshape(N, 1, 1)
    for k in ("x",): d[k] = (d[k].astype(np.float32) * f).astype(d[k].dtype)
    return d
def reference(x, w1, w3, w2):
    X, W1, W3, W2 = x.astype(np.float64), w1.astype(np.float64), w3.astype(np.float64), w2.astype(np.float64)
    y = np.zeros((N, 128, TK))
    for r in range(N):
        for j in range(N):
            y[r] += W2[j].T @ (silu(W1[j].T @ X[r]) * (W3[j].T @ X[r]))
    return {"y": y.astype(ml_dtypes.bfloat16)}

@@ -1,0 +1,137 @@
+from concourse.bass import DstId, RemoteDMATransfer
+from concourse.mybir import AluOpType, ActivationFunctionType
+
+TK = 32
+D = 128
+
+SCRATCH = {
+    "xs": ("sbuf", [128, 4 * TK], "bfloat16"),
+    "wo": ("sbuf", [128, 3 * D], "bfloat16"),
+    "wp": ("sbuf", [128, 3 * D], "bfloat16"),
+    "s0": ("sbuf", [128, 4 * TK], "float32"),
+    "s1": ("sbuf", [128, 4 * TK], "float32"),
+    "h0": ("sbuf", [128, 4 * TK], "bfloat16"),
+    "h1": ("sbuf", [128, 4 * TK], "bfloat16"),
+    "part": ("sbuf", [128, 3 * TK], "bfloat16"),
+    "acc": ("sbuf", [128, 4 * TK], "bfloat16"),
+    "t": ("sbuf", [128, 2 * TK], "float32"),
+    "ysb": ("sbuf", [128, TK], "bfloat16"),
+    "p1": ("psum", [128, 512], "float32"),
+    "p3": ("psum", [128, 512], "float32"),
+    "py": ("psum", [128, 512], "float32"),
+}
+SEMAPHORES = ["xld", "wld", "xarr", "warr", "parr", "sent", "yst",
+              "p1o", "p3o", "p1a", "p3a", "p1b", "p3b", "s0o", "s0a", "s1b", "h0o", "h0a", "h1b",
+              "ydone", "ev", "own", "tsum", "ybf"]
+
+
+def _bits(mask):
+    return [1 << b for b in range(mask.bit_length()) if (mask >> b) & 1]
+
+
+def rank_program(g, core, T, topo):
+    if T.rank_of(core) is None:
+        return
+    S = T.sem
+    silu = ActivationFunctionType.Silu
+    rack = topo.rack(topo.host(core))
+    group = [c for c in T.cores if topo.rack(topo.host(c)) == rack]
+    partner = [c for c in T.cores if topo.rack(topo.host(c)) != rack and topo.may_write(core, c)
+               and topo.chip(c) == topo.chip(core)][0]
+    G = len(group)
+    me = group.index(core)
+    peer = {s: group[(me + s) % G] for s in range(1, G)}
+
+    def dst(c):
+        rid, pid = topo.addr(c, core)
+        return DstId(rid=rid, pnc=pid)
+
+    def slot(buf, s, n=1):
+        return buf[:, s * TK:(s + n) * TK]
+
+    w1o, w3o, w2o = T.wo[:, 0:D], T.wo[:, D:2 * D], T.wo[:, 2 * D:3 * D]
+    w1p, w3p, w2p = T.wp[:, 0:D], T.wp[:, D:2 * D], T.wp[:, 2 * D:3 * D]
+
+    g.sync.dma_start(slot(T.xs, 0), T.x[:]).then_inc(S.xld, 16)
+    g.scalar.dma_start(w1o, T.w1[:]).then_inc(S.wld, 16)
+    g.sync.dma_start(w3o, T.w3[:]).then_inc(S.wld, 16)
+    g.scalar.dma_start(w2o, T.w2[:]).then_inc(S.wld, 16)
+
+    sent = 0
+    xmask = topo.mask(core, peer[1])
+    for s in peer:
+        xmask &= topo.mask(core, peer[s])
+    eng = _bits(xmask)
+    g.wait_ge(S.xld, 16)
+    g.remote_dma_fused([RemoteDMATransfer(
+        dst_ids=[dst(peer[s]) for s in peer], dma_engine_mask=xmask, remote_sem=S.xarr,
+        srcs=[slot(T.xs, 0)], dsts=[slot(T.xs, G - s) for s in peer], alu_op=0)], local_sem=S.sent)
+    sent += len(eng)
+
+    wmask = topo.mask(core, partner)
+    rid, pid = topo.addr(partner, core)
+    g.wait_ge(S.wld, 48)
+    g.remote_dma(T.wp[:], T.wo[:], S.warr, S.sent, pid, rid, wmask)
+    sent += len(_bits(wmask))
+
+    half = len(eng) // 2
+    lo, hi = sum(eng[:half]), sum(eng[half:])
+    g.wait_ge(S.ev, 1)
+    g.remote_dma_fused([
+        RemoteDMATransfer(dst_ids=[dst(peer[1])], dma_engine_mask=lo, remote_sem=S.parr,
+                          srcs=[slot(T.part, 0)], dsts=[slot(T.acc, G - 1)], alu_op=0),
+        RemoteDMATransfer(dst_ids=[dst(peer[2])], dma_engine_mask=hi, remote_sem=S.parr,
+                          srcs=[slot(T.part, 1)], dsts=[slot(T.acc, G - 2)], alu_op=0)], local_sem=S.sent)
+    sent += len(eng)
+    rid, pid = topo.addr(peer[3], core)
+    g.remote_dma(slot(T.acc, G - 3), slot(T.part, 2), S.parr, S.sent, pid, rid, xmask)
+    sent += len(eng)
+    g.wait_ge(S.sent, sent)
+
+    pe = g.tensor
+    pe.wait_ge(S.xld, 16)
+    pe.wait_ge(S.wld, 48)
+    pe.matmul(slot(T.p1, 0), w1o, slot(T.xs, 0), True, True).then_inc(S.p1o, 1)
+    pe.matmul(slot(T.p3, 0), w3o, slot(T.xs, 0), True, True).then_inc(S.p3o, 1)
+    pe.wait_ge(S.xarr, (G - 1) * len(eng))
+    pe.wait_ge(S.h0o, 1)
+    pe.matmul(slot(T.p1, 1, 3), w1o, slot(T.xs, 1, 3), True, True).then_inc(S.p1a, 1)
+    pe.matmul(slot(T.p3, 1, 3), w3o, slot(T.xs, 1, 3), True, True).then_inc(S.p3a, 1)
+    pe.wait_ge(S.h0a, 1)
+    pe.matmul(slot(T.py, 0, 4), w2o, T.h0[:], True, False)
+    pe.wait_ge(S.warr, len(_bits(wmask)))
+    pe.matmul(slot(T.p1, 0, 4), w1p, T.xs[:], True, True).then_inc(S.p1b, 1)
+    pe.matmul(slot(T.p3, 0, 4), w3p, T.xs[:], True, True).then_inc(S.p3b, 1)
+    pe.wait_ge(S.h1b, 1)
+    pe.matmul(slot(T.py, 0, 4), w2p, T.h1[:], False, True).then_inc(S.ydone, 1)
+
+    act = g.scalar
+    act.wait_ge(S.p1o, 1)
+    act.activation(slot(T.s0, 0), slot(T.p1, 0), silu).then_inc(S.s0o, 1)
+    act.wait_ge(S.p1a, 1)
+    act.activation(slot(T.s0, 1, 3), slot(T.p1, 1, 3), silu).then_inc(S.s0a, 1)
+    act.wait_ge(S.p1b, 1)
+    act.activation(T.s1[:], slot(T.p1, 0, 4), silu).then_inc(S.s1b, 1)
+
+    v = g.vector
+    v.wait_ge(S.s0o, 1)
+    v.wait_ge(S.p3o, 1)
+    v.tensor_tensor(slot(T.h0, 0), slot(T.s0, 0), slot(T.p3, 0), AluOpType.mult).then_inc(S.h0o, 1)
+    v.wait_ge(S.s0a, 1)
+    v.wait_ge(S.p3a, 1)
+    v.tensor_tensor(slot(T.h0, 1, 3), slot(T.s0, 1, 3), slot(T.p3, 1, 3), AluOpType.mult).then_inc(S.h0a, 1)
+    v.wait_ge(S.s1b, 1)
+    v.wait_ge(S.p3b, 1)
+    v.tensor_tensor(T.h1[:], T.s1[:], slot(T.p3, 0, 4), AluOpType.mult).then_inc(S.h1b, 1)
+    v.wait_ge(S.ydone, 1)
+    v.tensor_copy(T.part[:], slot(T.py, 1, 3)).then_inc(S.ev, 1)
+    v.tensor_copy(slot(T.acc, 0), slot(T.py, 0)).then_inc(S.own, 1)
+    v.wait_ge(S.own, 1)
+    v.wait_ge(S.parr, 2 * half + len(eng))
+    v.tensor_tensor(T.t[:], slot(T.acc, 0, 2), slot(T.acc, 2, 2), AluOpType.add).then_inc(S.tsum, 1)
+    v.wait_ge(S.tsum, 1)
+    v.tensor_tensor(T.ysb[:], slot(T.t, 0), slot(T.t, 1), AluOpType.add).then_inc(S.ybf, 1)
+
+    g.sync.wait_ge(S.ybf, 1)
+    g.sync.dma_start(T.y[:], T.ysb[:]).then_inc(S.yst, 16)
+    g.sync.wait_ge(S.yst, 16)

@@ -35,8 +35,9 @@ def rank_program(g, core, T, topo):
     S = T.sem
     silu = ActivationFunctionType.Silu
     rack = topo.rack(topo.host(core))
-    group = [c for c in T.cores if topo.rack(topo.host(c)) == rack]
-    partner = [c for c in T.cores if topo.rack(topo.host(c)) != rack and topo.may_write(core, c)
+    group = [c for c in T.cores if topo.host(c) == topo.host(core)
+             or (topo.rack(topo.host(c)) != rack and topo.may_write(core, c))]
+    partner = [c for c in T.cores if topo.same_plane(core, c) and topo.host(c) != topo.host(core)
                and topo.chip(c) == topo.chip(core)][0]
     G = len(group)
     me = group.index(core)

@@ -8,21 +8,29 @@ SCRATCH = {
     "xs": ("sbuf", [128, 4 * TK], "bfloat16"),
     "wo": ("sbuf", [128, 3 * D], "bfloat16"),
     "wp": ("sbuf", [128, 3 * D], "bfloat16"),
-    "s0": ("sbuf", [128, 4 * TK], "float32"),
-    "s1": ("sbuf", [128, 4 * TK], "float32"),
-    "h0": ("sbuf", [128, 4 * TK], "bfloat16"),
-    "h1": ("sbuf", [128, 4 * TK], "bfloat16"),
-    "part": ("sbuf", [128, 3 * TK], "bfloat16"),
-    "acc": ("sbuf", [128, 4 * TK], "bfloat16"),
-    "t": ("sbuf", [128, 2 * TK], "float32"),
+    "s0": ("sbuf", [128, 3 * TK], "float32"),
+    "s1": ("sbuf", [128, 3 * TK], "float32"),
+    "sn": ("sbuf", [128, 2 * TK], "float32"),
+    "h0": ("sbuf", [128, 3 * TK], "bfloat16"),
+    "h1": ("sbuf", [128, 3 * TK], "bfloat16"),
+    "hn": ("sbuf", [128, 2 * TK], "bfloat16"),
+    "parta": ("sbuf", [128, 2 * TK], "bfloat16"),
+    "partb": ("sbuf", [128, TK], "bfloat16"),
+    "acca": ("sbuf", [128, 2 * TK], "bfloat16"),
+    "accb": ("sbuf", [128, TK], "bfloat16"),
+    "e1": ("sbuf", [128, TK], "float32"),
+    "e2": ("sbuf", [128, TK], "float32"),
     "ysb": ("sbuf", [128, TK], "bfloat16"),
-    "p1": ("psum", [128, 512], "float32"),
-    "p3": ("psum", [128, 512], "float32"),
+    "p1a": ("psum", [128, 512], "float32"),
+    "p3a": ("psum", [128, 512], "float32"),
+    "p1b": ("psum", [128, 512], "float32"),
+    "p3b": ("psum", [128, 512], "float32"),
     "py": ("psum", [128, 512], "float32"),
+    "pyn": ("psum", [128, 512], "float32"),
 }
-SEMAPHORES = ["xld", "wld", "xarr", "warr", "parr", "sent", "yst",
-              "p1o", "p3o", "p1a", "p3a", "p1b", "p3b", "s0o", "s0a", "s1b", "h0o", "h0a", "h1b",
-              "ydone", "ev", "own", "tsum", "ybf"]
+SEMAPHORES = ["xld", "wld", "xarra", "xarrn", "warr", "parra", "parrb", "sent", "yst",
+              "p1o", "p3o", "p1a", "p3a", "p1b", "p3b", "p1n", "p3n", "s0o", "s0a", "s1b", "snd",
+              "h0o", "h0a", "h1b", "hnd", "ydone", "yndone", "eva", "evb", "e1d", "e2d", "ybf"]
 
 
 def _bits(mask):
@@ -34,14 +42,15 @@ def rank_program(g, core, T, topo):
         return
     S = T.sem
     silu = ActivationFunctionType.Silu
+    mult, add = AluOpType.mult, AluOpType.add
     rack = topo.rack(topo.host(core))
-    group = [c for c in T.cores if topo.host(c) == topo.host(core)
-             or (topo.rack(topo.host(c)) != rack and topo.may_write(core, c))]
-    partner = [c for c in T.cores if topo.same_plane(core, c) and topo.host(c) != topo.host(core)
+    others = [c for c in T.cores if c != core]
+    near = [c for c in others if topo.host(c) == topo.host(core)][0]
+    over = [c for c in others if topo.rack(topo.host(c)) != rack and topo.may_write(core, c)]
+    cab = [c for c in over if topo.chip(c) == topo.chip(core)][0]
+    far = [c for c in over if topo.chip(c) != topo.chip(core)][0]
+    partner = [c for c in others if topo.same_plane(core, c) and topo.host(c) != topo.host(core)
                and topo.chip(c) == topo.chip(core)][0]
-    G = len(group)
-    me = group.index(core)
-    peer = {s: group[(me + s) % G] for s in range(1, G)}
 
     def dst(c):
         rid, pid = topo.addr(c, core)
@@ -58,80 +67,97 @@ def rank_program(g, core, T, topo):
     g.sync.dma_start(w3o, T.w3[:]).then_inc(S.wld, 16)
     g.scalar.dma_start(w2o, T.w2[:]).then_inc(S.wld, 16)
 
+    allmask = topo.mask(core, partner)
+    for c in (near, cab, far):
+        allmask &= topo.mask(core, c)
+    eng = _bits(allmask)
+    weng, xeng = eng[0::2], eng[1::2]
     sent = 0
-    xmask = topo.mask(core, peer[1])
-    for s in peer:
-        xmask &= topo.mask(core, peer[s])
-    eng = _bits(xmask)
     g.wait_ge(S.xld, 16)
     g.remote_dma_fused([RemoteDMATransfer(
-        dst_ids=[dst(peer[s]) for s in peer], dma_engine_mask=xmask, remote_sem=S.xarr,
-        srcs=[slot(T.xs, 0)], dsts=[slot(T.xs, G - s) for s in peer], alu_op=0)], local_sem=S.sent)
-    sent += len(eng)
-
-    wmask = topo.mask(core, partner)
+        dst_ids=[dst(far), dst(cab)], dma_engine_mask=sum(xeng), remote_sem=S.xarra,
+        srcs=[slot(T.xs, 0)], dsts=[slot(T.xs, 2), slot(T.xs, 1)], alu_op=0)], local_sem=S.sent)
+    sent += len(xeng)
     rid, pid = topo.addr(partner, core)
     g.wait_ge(S.wld, 48)
-    g.remote_dma(T.wp[:], T.wo[:], S.warr, S.sent, pid, rid, wmask)
-    sent += len(_bits(wmask))
-
+    g.remote_dma(T.wp[:], T.wo[:], S.warr, S.sent, pid, rid, sum(weng))
+    sent += len(weng)
+    rid, pid = topo.addr(near, core)
+    g.remote_dma(slot(T.xs, 3), slot(T.xs, 0), S.xarrn, S.sent, pid, rid, sum(xeng))
+    sent += len(xeng)
     half = len(eng) // 2
     lo, hi = sum(eng[:half]), sum(eng[half:])
-    g.wait_ge(S.ev, 1)
+    g.wait_ge(S.eva, 1)
     g.remote_dma_fused([
-        RemoteDMATransfer(dst_ids=[dst(peer[1])], dma_engine_mask=lo, remote_sem=S.parr,
-                          srcs=[slot(T.part, 0)], dsts=[slot(T.acc, G - 1)], alu_op=0),
-        RemoteDMATransfer(dst_ids=[dst(peer[2])], dma_engine_mask=hi, remote_sem=S.parr,
-                          srcs=[slot(T.part, 1)], dsts=[slot(T.acc, G - 2)], alu_op=0)], local_sem=S.sent)
+        RemoteDMATransfer(dst_ids=[dst(far)], dma_engine_mask=lo, remote_sem=S.parra,
+                          srcs=[slot(T.parta, 1)], dsts=[slot(T.acca, 1)], alu_op=0),
+        RemoteDMATransfer(dst_ids=[dst(cab)], dma_engine_mask=hi, remote_sem=S.parra,
+                          srcs=[slot(T.parta, 0)], dsts=[slot(T.acca, 0)], alu_op=0)], local_sem=S.sent)
     sent += len(eng)
-    rid, pid = topo.addr(peer[3], core)
-    g.remote_dma(slot(T.acc, G - 3), slot(T.part, 2), S.parr, S.sent, pid, rid, xmask)
+    g.wait_ge(S.evb, 1)
+    g.remote_dma(T.accb[:], T.partb[:], S.parrb, S.sent, pid, rid, allmask)
     sent += len(eng)
     g.wait_ge(S.sent, sent)
 
     pe = g.tensor
     pe.wait_ge(S.xld, 16)
     pe.wait_ge(S.wld, 48)
-    pe.matmul(slot(T.p1, 0), w1o, slot(T.xs, 0), True, True).then_inc(S.p1o, 1)
-    pe.matmul(slot(T.p3, 0), w3o, slot(T.xs, 0), True, True).then_inc(S.p3o, 1)
-    pe.wait_ge(S.xarr, (G - 1) * len(eng))
+    pe.matmul(slot(T.p1a, 0), w1o, slot(T.xs, 0), True, True).then_inc(S.p1o, 1)
+    pe.matmul(slot(T.p3a, 0), w3o, slot(T.xs, 0), True, True).then_inc(S.p3o, 1)
+    pe.wait_ge(S.xarra, 2 * len(xeng))
     pe.wait_ge(S.h0o, 1)
-    pe.matmul(slot(T.p1, 1, 3), w1o, slot(T.xs, 1, 3), True, True).then_inc(S.p1a, 1)
-    pe.matmul(slot(T.p3, 1, 3), w3o, slot(T.xs, 1, 3), True, True).then_inc(S.p3a, 1)
+    pe.matmul(slot(T.p1a, 1, 2), w1o, slot(T.xs, 1, 2), True, True).then_inc(S.p1a, 1)
+    pe.matmul(slot(T.p3a, 1, 2), w3o, slot(T.xs, 1, 2), True, True).then_inc(S.p3a, 1)
+    pe.wait_ge(S.warr, len(weng))
+    pe.matmul(slot(T.p1b, 0, 3), w1p, slot(T.xs, 0, 3), True, True).then_inc(S.p1b, 1)
+    pe.matmul(slot(T.p3b, 0, 3), w3p, slot(T.xs, 0, 3), True, True).then_inc(S.p3b, 1)
     pe.wait_ge(S.h0a, 1)
-    pe.matmul(slot(T.py, 0, 4), w2o, T.h0[:], True, False)
-    pe.wait_ge(S.warr, len(_bits(wmask)))
-    pe.matmul(slot(T.p1, 0, 4), w1p, T.xs[:], True, True).then_inc(S.p1b, 1)
-    pe.matmul(slot(T.p3, 0, 4), w3p, T.xs[:], True, True).then_inc(S.p3b, 1)
+    pe.matmul(slot(T.py, 0, 3), w2o, T.h0[:], True, False)
     pe.wait_ge(S.h1b, 1)
-    pe.matmul(slot(T.py, 0, 4), w2p, T.h1[:], False, True).then_inc(S.ydone, 1)
+    pe.matmul(slot(T.py, 0, 3), w2p, T.h1[:], False, True).then_inc(S.ydone, 1)
+    pe.wait_ge(S.xarrn, len(xeng))
+    pe.matmul(slot(T.p1a, 4), w1o, slot(T.xs, 3), True, True).then_inc(S.p1n, 1)
+    pe.matmul(slot(T.p1a, 5), w1p, slot(T.xs, 3), True, True).then_inc(S.p1n, 1)
+    pe.matmul(slot(T.p3a, 4), w3o, slot(T.xs, 3), True, True).then_inc(S.p3n, 1)
+    pe.matmul(slot(T.p3a, 5), w3p, slot(T.xs, 3), True, True).then_inc(S.p3n, 1)
+    pe.wait_ge(S.hnd, 1)
+    pe.matmul(slot(T.pyn, 0), w2o, slot(T.hn, 0), True, False)
+    pe.matmul(slot(T.pyn, 0), w2p, slot(T.hn, 1), False, True).then_inc(S.yndone, 1)
 
     act = g.scalar
     act.wait_ge(S.p1o, 1)
-    act.activation(slot(T.s0, 0), slot(T.p1, 0), silu).then_inc(S.s0o, 1)
+    act.activation(slot(T.s0, 0), slot(T.p1a, 0), silu).then_inc(S.s0o, 1)
     act.wait_ge(S.p1a, 1)
-    act.activation(slot(T.s0, 1, 3), slot(T.p1, 1, 3), silu).then_inc(S.s0a, 1)
+    act.activation(slot(T.s0, 1, 2), slot(T.p1a, 1, 2), silu).then_inc(S.s0a, 1)
     act.wait_ge(S.p1b, 1)
-    act.activation(T.s1[:], slot(T.p1, 0, 4), silu).then_inc(S.s1b, 1)
+    act.activation(T.s1[:], slot(T.p1b, 0, 3), silu).then_inc(S.s1b, 1)
+    act.wait_ge(S.p1n, 2)
+    act.activation(T.sn[:], slot(T.p1a, 4, 2), silu).then_inc(S.snd, 1)
 
     v = g.vector
     v.wait_ge(S.s0o, 1)
     v.wait_ge(S.p3o, 1)
-    v.tensor_tensor(slot(T.h0, 0), slot(T.s0, 0), slot(T.p3, 0), AluOpType.mult).then_inc(S.h0o, 1)
+    v.tensor_tensor(slot(T.h0, 0), slot(T.s0, 0), slot(T.p3a, 0), mult).then_inc(S.h0o, 1)
     v.wait_ge(S.s0a, 1)
     v.wait_ge(S.p3a, 1)
-    v.tensor_tensor(slot(T.h0, 1, 3), slot(T.s0, 1, 3), slot(T.p3, 1, 3), AluOpType.mult).then_inc(S.h0a, 1)
+    v.tensor_tensor(slot(T.h0, 1, 2), slot(T.s0, 1, 2), slot(T.p3a, 1, 2), mult).then_inc(S.h0a, 1)
     v.wait_ge(S.s1b, 1)
     v.wait_ge(S.p3b, 1)
-    v.tensor_tensor(T.h1[:], T.s1[:], slot(T.p3, 0, 4), AluOpType.mult).then_inc(S.h1b, 1)
+    v.tensor_tensor(T.h1[:], T.s1[:], slot(T.p3b, 0, 3), mult).then_inc(S.h1b, 1)
     v.wait_ge(S.ydone, 1)
-    v.tensor_copy(T.part[:], slot(T.py, 1, 3)).then_inc(S.ev, 1)
-    v.tensor_copy(slot(T.acc, 0), slot(T.py, 0)).then_inc(S.own, 1)
-    v.wait_ge(S.own, 1)
-    v.wait_ge(S.parr, 2 * half + len(eng))
-    v.tensor_tensor(T.t[:], slot(T.acc, 0, 2), slot(T.acc, 2, 2), AluOpType.add).then_inc(S.tsum, 1)
-    v.wait_ge(S.tsum, 1)
-    v.tensor_tensor(T.ysb[:], slot(T.t, 0), slot(T.t, 1), AluOpType.add).then_inc(S.ybf, 1)
+    v.tensor_copy(T.parta[:], slot(T.py, 1, 2)).then_inc(S.eva, 1)
+    v.wait_ge(S.snd, 1)
+    v.wait_ge(S.p3n, 2)
+    v.tensor_tensor(T.hn[:], T.sn[:], slot(T.p3a, 4, 2), mult).then_inc(S.hnd, 1)
+    v.wait_ge(S.yndone, 1)
+    v.tensor_copy(T.partb[:], slot(T.pyn, 0)).then_inc(S.evb, 1)
+    v.wait_ge(S.parra, 2 * half)
+    v.tensor_tensor(T.e1[:], slot(T.acca, 0), slot(T.acca, 1), add).then_inc(S.e1d, 1)
+    v.wait_ge(S.e1d, 1)
+    v.tensor_tensor(T.e2[:], T.e1[:], slot(T.py, 0), add).then_inc(S.e2d, 1)
+    v.wait_ge(S.e2d, 1)
+    v.wait_ge(S.parrb, len(eng))
+    v.tensor_tensor(T.ysb[:], T.e2[:], T.accb[:], add).then_inc(S.ybf, 1)
 
     g.sync.wait_ge(S.ybf, 1)
     g.sync.dma_start(T.y[:], T.ysb[:]).then_inc(S.yst, 16)

from concourse.bass import DstId, RemoteDMATransfer
from concourse.mybir import AluOpType, ActivationFunctionType

TK = 32
D = 128

SCRATCH = {
    "xs": ("sbuf", [128, 4 * TK], "bfloat16"),
    "wo": ("sbuf", [128, 3 * D], "bfloat16"),
    "wp": ("sbuf", [128, 3 * D], "bfloat16"),
    "s0": ("sbuf", [128, 3 * TK], "float32"),
    "s1": ("sbuf", [128, 3 * TK], "float32"),
    "sn": ("sbuf", [128, 2 * TK], "float32"),
    "h0": ("sbuf", [128, 3 * TK], "bfloat16"),
    "h1": ("sbuf", [128, 3 * TK], "bfloat16"),
    "hn": ("sbuf", [128, 2 * TK], "bfloat16"),
    "parta": ("sbuf", [128, 2 * TK], "bfloat16"),
    "partb": ("sbuf", [128, TK], "bfloat16"),
    "acca": ("sbuf", [128, 2 * TK], "bfloat16"),
    "accb": ("sbuf", [128, TK], "bfloat16"),
    "e1": ("sbuf", [128, TK], "float32"),
    "e2": ("sbuf", [128, TK], "float32"),
    "ysb": ("sbuf", [128, TK], "bfloat16"),
    "p1a": ("psum", [128, 512], "float32"),
    "p3a": ("psum", [128, 512], "float32"),
    "p1b": ("psum", [128, 512], "float32"),
    "p3b": ("psum", [128, 512], "float32"),
    "py": ("psum", [128, 512], "float32"),
    "pyn": ("psum", [128, 512], "float32"),
}
SEMAPHORES = ["xld", "wld", "xarra", "xarrn", "warr", "parra", "parrb", "sent", "yst",
              "p1o", "p3o", "p1a", "p3a", "p1b", "p3b", "p1n", "p3n", "s0o", "s0a", "s1b", "snd",
              "h0o", "h0a", "h1b", "hnd", "ydone", "yndone", "eva", "evb", "e1d", "e2d", "ybf"]


def _bits(mask):
    return [1 << b for b in range(mask.bit_length()) if (mask >> b) & 1]


def rank_program(g, core, T, topo):
    if T.rank_of(core) is None:
        return
    S = T.sem
    silu = ActivationFunctionType.Silu
    mult, add = AluOpType.mult, AluOpType.add
    rack = topo.rack(topo.host(core))
    others = [c for c in T.cores if c != core]
    near = [c for c in others if topo.host(c) == topo.host(core)][0]
    over = [c for c in others if topo.rack(topo.host(c)) != rack and topo.may_write(core, c)]
    cab = [c for c in over if topo.chip(c) == topo.chip(core)][0]
    far = [c for c in over if topo.chip(c) != topo.chip(core)][0]
    partner = [c for c in others if topo.same_plane(core, c) and topo.host(c) != topo.host(core)
               and topo.chip(c) == topo.chip(core)][0]

    def dst(c):
        rid, pid = topo.addr(c, core)
        return DstId(rid=rid, pnc=pid)

    def slot(buf, s, n=1):
        return buf[:, s * TK:(s + n) * TK]

    w1o, w3o, w2o = T.wo[:, 0:D], T.wo[:, D:2 * D], T.wo[:, 2 * D:3 * D]
    w1p, w3p, w2p = T.wp[:, 0:D], T.wp[:, D:2 * D], T.wp[:, 2 * D:3 * D]

    g.sync.dma_start(slot(T.xs, 0), T.x[:]).then_inc(S.xld, 16)
    g.scalar.dma_start(w1o, T.w1[:]).then_inc(S.wld, 16)
    g.sync.dma_start(w3o, T.w3[:]).then_inc(S.wld, 16)
    g.scalar.dma_start(w2o, T.w2[:]).then_inc(S.wld, 16)

    allmask = topo.mask(core, partner)
    for c in (near, cab, far):
        allmask &= topo.mask(core, c)
    eng = _bits(allmask)
    weng, xeng = eng[0::2], eng[1::2]
    sent = 0
    g.wait_ge(S.xld, 16)
    g.remote_dma_fused([RemoteDMATransfer(
        dst_ids=[dst(far), dst(cab)], dma_engine_mask=sum(xeng), remote_sem=S.xarra,
        srcs=[slot(T.xs, 0)], dsts=[slot(T.xs, 2), slot(T.xs, 1)], alu_op=0)], local_sem=S.sent)
    sent += len(xeng)
    rid, pid = topo.addr(partner, core)
    g.wait_ge(S.wld, 48)
    g.remote_dma(T.wp[:], T.wo[:], S.warr, S.sent, pid, rid, sum(weng))
    sent += len(weng)
    rid, pid = topo.addr(near, core)
    g.remote_dma(slot(T.xs, 3), slot(T.xs, 0), S.xarrn, S.sent, pid, rid, sum(xeng))
    sent += len(xeng)
    half = len(eng) // 2
    lo, hi = sum(eng[:half]), sum(eng[half:])
    g.wait_ge(S.eva, 1)
    g.remote_dma_fused([
        RemoteDMATransfer(dst_ids=[dst(far)], dma_engine_mask=lo, remote_sem=S.parra,
                          srcs=[slot(T.parta, 1)], dsts=[slot(T.acca, 1)], alu_op=0),
        RemoteDMATransfer(dst_ids=[dst(cab)], dma_engine_mask=hi, remote_sem=S.parra,
                          srcs=[slot(T.parta, 0)], dsts=[slot(T.acca, 0)], alu_op=0)], local_sem=S.sent)
    sent += len(eng)
    g.wait_ge(S.evb, 1)
    g.remote_dma(T.accb[:], T.partb[:], S.parrb, S.sent, pid, rid, allmask)
    sent += len(eng)
    g.wait_ge(S.sent, sent)

    pe = g.tensor
    pe.wait_ge(S.xld, 16)
    pe.wait_ge(S.wld, 48)
    pe.matmul(slot(T.p1a, 0), w1o, slot(T.xs, 0), True, True).then_inc(S.p1o, 1)
    pe.matmul(slot(T.p3a, 0), w3o, slot(T.xs, 0), True, True).then_inc(S.p3o, 1)
    pe.wait_ge(S.xarra, 2 * len(xeng))
    pe.wait_ge(S.h0o, 1)
    pe.matmul(slot(T.p1a, 1, 2), w1o, slot(T.xs, 1, 2), True, True).then_inc(S.p1a, 1)
    pe.matmul(slot(T.p3a, 1, 2), w3o, slot(T.xs, 1, 2), True, True).then_inc(S.p3a, 1)
    pe.wait_ge(S.warr, len(weng))
    pe.matmul(slot(T.p1b, 0, 3), w1p, slot(T.xs, 0, 3), True, True).then_inc(S.p1b, 1)
    pe.matmul(slot(T.p3b, 0, 3), w3p, slot(T.xs, 0, 3), True, True).then_inc(S.p3b, 1)
    pe.wait_ge(S.h0a, 1)
    pe.matmul(slot(T.py, 0, 3), w2o, T.h0[:], True, False)
    pe.wait_ge(S.h1b, 1)
    pe.matmul(slot(T.py, 0, 3), w2p, T.h1[:], False, True).then_inc(S.ydone, 1)
    pe.wait_ge(S.xarrn, len(xeng))
    pe.matmul(slot(T.p1a, 4), w1o, slot(T.xs, 3), True, True).then_inc(S.p1n, 1)
    pe.matmul(slot(T.p1a, 5), w1p, slot(T.xs, 3), True, True).then_inc(S.p1n, 1)
    pe.matmul(slot(T.p3a, 4), w3o, slot(T.xs, 3), True, True).then_inc(S.p3n, 1)
    pe.matmul(slot(T.p3a, 5), w3p, slot(T.xs, 3), True, True).then_inc(S.p3n, 1)
    pe.wait_ge(S.hnd, 1)
    pe.matmul(slot(T.pyn, 0), w2o, slot(T.hn, 0), True, False)
    pe.matmul(slot(T.pyn, 0), w2p, slot(T.hn, 1), False, True).then_inc(S.yndone, 1)

    act = g.scalar
    act.wait_ge(S.p1o, 1)
    act.activation(slot(T.s0, 0), slot(T.p1a, 0), silu).then_inc(S.s0o, 1)
    act.wait_ge(S.p1a, 1)
    act.activation(slot(T.s0, 1, 2), slot(T.p1a, 1, 2), silu).then_inc(S.s0a, 1)
    act.wait_ge(S.p1b, 1)
    act.activation(T.s1[:], slot(T.p1b, 0, 3), silu).then_inc(S.s1b, 1)
    act.wait_ge(S.p1n, 2)
    act.activation(T.sn[:], slot(T.p1a, 4, 2), silu).then_inc(S.snd, 1)

    v = g.vector
    v.wait_ge(S.s0o, 1)
    v.wait_ge(S.p3o, 1)
    v.tensor_tensor(slot(T.h0, 0), slot(T.s0, 0), slot(T.p3a, 0), mult).then_inc(S.h0o, 1)
    v.wait_ge(S.s0a, 1)
    v.wait_ge(S.p3a, 1)
    v.tensor_tensor(slot(T.h0, 1, 2), slot(T.s0, 1, 2), slot(T.p3a, 1, 2), mult).then_inc(S.h0a, 1)
    v.wait_ge(S.s1b, 1)
    v.wait_ge(S.p3b, 1)
    v.tensor_tensor(T.h1[:], T.s1[:], slot(T.p3b, 0, 3), mult).then_inc(S.h1b, 1)
    v.wait_ge(S.ydone, 1)
    v.tensor_copy(T.parta[:], slot(T.py, 1, 2)).then_inc(S.eva, 1)
    v.wait_ge(S.snd, 1)
    v.wait_ge(S.p3n, 2)
    v.tensor_tensor(T.hn[:], T.sn[:], slot(T.p3a, 4, 2), mult).then_inc(S.hnd, 1)
    v.wait_ge(S.yndone, 1)
    v.tensor_copy(T.partb[:], slot(T.pyn, 0)).then_inc(S.evb, 1)
    v.wait_ge(S.parra, 2 * half)
    v.tensor_tensor(T.e1[:], slot(T.acca, 0), slot(T.acca, 1), add).then_inc(S.e1d, 1)
    v.wait_ge(S.e1d, 1)
    v.tensor_tensor(T.e2[:], T.e1[:], slot(T.py, 0), add).then_inc(S.e2d, 1)
    v.wait_ge(S.e2d, 1)
    v.wait_ge(S.parrb, len(eng))
    v.tensor_tensor(T.ysb[:], T.e2[:], T.accb[:], add).then_inc(S.ybf, 1)

    g.sync.wait_ge(S.ybf, 1)
    g.sync.dma_start(T.y[:], T.ysb[:]).then_inc(S.yst, 16)
    g.sync.wait_ge(S.yst, 16)
